import numpy as np
import ml_dtypes


def mxq(x, axis, fmt="e4m3"):
    dtype, down = {"e4m3": (ml_dtypes.float8_e4m3fn, 7), "e5m2": (ml_dtypes.float8_e5m2, 14)}[fmt]
    v = np.moveaxis(np.asarray(x, np.float32).astype(ml_dtypes.bfloat16).astype(np.float64), axis, -1)
    blocks = v.reshape(v.shape[:-1] + (-1, 32))
    amax = np.abs(blocks).max(-1, keepdims=True)
    byte = np.maximum(np.where(amax > 0, np.frexp(amax)[1] - 1 + 127, 0) - down, 1)
    scale = np.exp2(byte - 127.0)
    codes = (blocks / scale).astype(np.float32).astype(dtype).astype(np.float64)
    return np.moveaxis((codes * scale).reshape(v.shape), -1, axis)


WIDE = False


def mx_kscale(k):
    if not WIDE:
        return np.ones(k)
    levels = np.array([10, -10, 5, -5, 0])
    if k % 512:
        return np.exp2(np.random.permutation(np.resize(levels, k // 32))).repeat(32)
    a = np.empty((k // 512, 16))
    for p in range(k // 512):
        a[p, :8] = np.random.permutation(np.resize(levels, 8))
        for g in range(8):
            far = levels[np.abs(levels - a[p, g]) >= 10]
            a[p, g + 8] = far[np.random.randint(len(far))]
    return np.exp2(a.ravel()).repeat(32)


BF16 = ml_dtypes.bfloat16


def bf(x):
    return np.asarray(x, np.float32).astype(BF16)


def f64(x):
    return np.asarray(x).astype(np.float64)


E2M1 = np.array([0.0, 0.5, 1.0, 1.5, 2.0, 3.0, 4.0, 6.0, -0.0, -0.5, -1.0, -1.5, -2.0, -3.0, -4.0, -6.0])


def pack_weight(w, fmt):
    k, n = w.shape
    w = f64(bf(w)).reshape(k // 32, 32, n)
    amax = np.abs(w).max(1)
    if fmt == "e4m3":
        byte = np.frexp(amax)[1] - 1 + 127 - 7
    else:
        mant, ex = np.frexp(amax / 6.0)
        byte = np.where(mant > 0.5, ex, ex - 1) + 127
    byte = np.clip(np.where(amax > 0, byte, 1), 1, 254)
    scaled = (w * np.exp2(127.0 - byte)[:, None, :]).reshape(k, n).astype(np.float32)
    by_word = np.ascontiguousarray(scaled.reshape(k // 512, 128, 4, n).transpose(0, 1, 3, 2))
    if fmt == "e4m3":
        words = by_word.astype(ml_dtypes.float8_e4m3fn).view(np.uint8)
    else:
        c = by_word.astype(ml_dtypes.float4_e2m1fn).view(np.uint8) & 0xF
        words = c[..., 0::2] | (c[..., 1::2] << 4)
    return np.ascontiguousarray(words), np.ascontiguousarray(byte.astype(np.uint8).reshape(k // 512, 16, n))


def unpack_weight(words, scales, fmt):
    g, p, n, _ = words.shape
    if fmt == "e4m3":
        vals = np.ascontiguousarray(words).view(ml_dtypes.float8_e4m3fn).astype(np.float64)
    else:
        nib = np.empty((g, p, n, 4), np.uint8)
        nib[..., 0::2] = words & 0xF
        nib[..., 1::2] = words >> 4
        vals = E2M1[nib]
    vals = vals * np.repeat(np.exp2(scales.astype(np.float64) - 127.0), 8, axis=1)[..., None]
    return vals.transpose(0, 1, 3, 2).reshape(g * 512, n)
def pack4(w):
    words, scales = pack_weight(w, "e2m1")
    return words.reshape(words.shape[0], 128, -1), scales


def unpack4(words, scales):
    return unpack_weight(words.reshape(words.shape[0], 128, -1, 2), scales, "e2m1")


M, N = 1024, 1536

AMP = 0.4
POT = 0.3


def setup_inputs():
    su = mx_kscale(M)
    sv = mx_kscale(N)
    solute = AMP * np.random.standard_normal((M, M)) / np.sqrt(M) * su
    dressed = np.random.standard_normal((M, N)) / su[:, None]
    direct = np.random.standard_normal((M, N)) * sv
    solvent = AMP * np.random.standard_normal((N, N)) / np.sqrt(N) / sv[:, None]
    d_words, d_scales = pack4(dressed)
    return {"solute": bf(solute),
            "d_words": d_words,
            "d_scales": d_scales,
            "direct": bf(direct),
            "solvent": bf(solvent),
            "potential": bf(POT * np.random.standard_normal((M, N)))}


def reference(solute, d_words, d_scales, direct, solvent, potential):
    left = mxq(f64(solute), 1, "e4m3") @ unpack4(d_words, d_scales)
    right = mxq(f64(direct), 1, "e4m3") @ mxq(f64(solvent), 0, "e4m3")
    tau = left + right
    pair = np.exp(tau - f64(potential))
    c_new = pair - 1.0 - tau
    return tau, c_new

@@ -1,0 +1,325 @@
+from contextlib import ExitStack
+
+import concourse.mybir as mybir
+from concourse.masks import make_identity
+
+M, N = 1024, 1536
+FLOPS = 2 * M * N * (M + N)
+
+F32 = mybir.dt.float32
+BF16 = mybir.dt.bfloat16
+I32 = mybir.dt.int32
+U32 = mybir.dt.uint32
+U8 = mybir.dt.uint8
+E4M3X4 = mybir.dt.float8_e4m3fn_x4
+E2M1X4 = mybir.dt.float4_e2m1fn_x4
+EXP = mybir.ActivationFunctionType.Exp
+SUB = mybir.AluOpType.subtract
+
+P = 128
+K_PASS = 512
+SU_PASSES = M // K_PASS
+SV_PASSES = N // K_PASS
+R = 2
+GROUPS = M // (P * R)
+N_TILE = 512
+N_TILES = N // N_TILE
+UNITS = R * (SU_PASSES + SV_PASSES)
+BANKS = UNITS // 2
+
+
+def tile_rism_hnc_update_s1_kernel(tc, solute, d_words, d_scales, direct, solvent, potential, tau_out, c_out):
+    nc = tc.nc
+    with ExitStack() as ctx:
+        keep = ctx.enter_context(tc.tile_pool(name="keep", bufs=1))
+        stage = ctx.enter_context(tc.tile_pool(name="stage", bufs=4))
+        psum = ctx.enter_context(tc.psum_pool(name="psum", bufs=1))
+
+        ident = keep.tile([P, P], F32, name="ident")
+        make_identity(nc, ident[:])
+        plane = keep.tile([P, SU_PASSES, N], U8, name="plane", align_bytes=64)
+        nc.vector.memset(plane[:].rearrange("p g n -> p (g n)").bitcast(I32), 0)
+        warm = keep.tile([P, 1], F32, name="warm")
+        nc.vector.memset(warm[:], 0.0)
+
+        su_rows = solute.rearrange("(h p r) k -> h p r k", p=P, r=R)
+        c_rows = direct.rearrange("(h p r) k -> h p r k", p=P, r=R)
+        u_rows = potential.rearrange("(h p r) n -> h p r n", p=P, r=R)
+        tau_rows = tau_out.rearrange("(h p r) n -> h p r n", p=P, r=R)
+        cnew_rows = c_out.rearrange("(h p r) n -> h p r n", p=P, r=R)
+        sv_rows = solvent.rearrange("(g p j) n -> g p j n", p=P, j=4)
+
+        su_raw = {}
+        c_raw = {}
+        u_raw = {}
+        sv_raw = {}
+        words = keep.tile([P, SU_PASSES, 2 * N], U8, name="words", align_bytes=64)
+
+        def load_su(h):
+            su_raw[h] = keep.tile([P, R, M], BF16, name=f"su_raw{h}")
+            nc.sync.dma_start(out=su_raw[h][:], in_=su_rows[h])
+
+        def load_c(h):
+            c_raw[h] = keep.tile([P, R, N], BF16, name=f"c_raw{h}")
+            nc.sync.dma_start(out=c_raw[h][:], in_=c_rows[h])
+
+        def load_u(h):
+            u_raw[h] = keep.tile([P, R, N], BF16, name=f"u_raw{h}")
+            nc.sync.dma_start(out=u_raw[h][:], in_=u_rows[h])
+
+        def load_sv(g, n0, n1):
+            cols = slice(n0 * N_TILE, n1 * N_TILE)
+            tile = keep.tile([P, 4, (n1 - n0) * N_TILE], BF16, name=f"sv_raw{g}_{n0}")
+            nc.sync.dma_start(out=tile[:], in_=sv_rows[g][:, :, cols])
+            for n in range(n0, n1):
+                sv_raw[g, n] = tile[:, :, (n - n0) * N_TILE : (n + 1 - n0) * N_TILE]
+
+        def load_d():
+            nc.sync.dma_start(
+                out=words[:].bitcast(I32), in_=d_words.rearrange("g p b -> p g b").bitcast(I32)
+            )
+
+        def load_d_scales():
+            for r in range(4):
+                nc.scalar.dma_start(
+                    out=plane[r:P:32, :, :].bitcast(I32),
+                    in_=d_scales.rearrange("g (q r) n -> r q g n", r=4)[r].bitcast(I32),
+                )
+
+        LOADS = "s0 v0 c0 d v1 s1 v2 c1 s2 u0 s3 c2 u1 c3 u2 u3".split()
+        PROG = "s0 v0 c0 E6 F6 v1 G6 s1 v2 c1 s2 s3 c2 c3".split()
+        BUFA = 6
+        BUFB = 3
+        V_IL = ('svv', 'vvs', 'vsv')
+        R0 = 'n'
+        NFINE = 3
+        SUMB = 6
+        EV = 's'
+        load_d_scales()
+        for it in LOADS:
+            k = int(it[1]) if len(it) > 1 else 0
+            if it[0] == "s":
+                load_su(k)
+            if it[0] == "c":
+                load_c(k)
+            if it[0] == "u":
+                load_u(k)
+            if it[0] == "v":
+                load_sv(k, 0, 3)
+            if it[0] == "d":
+                load_d()
+        nc.scalar.activation(out=warm[:], in_=warm[:], func=EXP)
+
+        row_codes = {}
+        row_scales = {}
+        for h in range(GROUPS):
+            row_codes[h] = keep.tile([P, UNITS, P], U32, name=f"row_codes{h}", align_bytes=64)
+            row_scales[h] = keep.tile([P, UNITS, P], U8, name=f"row_scales{h}", align_bytes=64)
+        sv_codes = keep.tile([P, SV_PASSES, N], U32, name="sv_codes", align_bytes=64)
+        sv_scales = keep.tile([P, SV_PASSES, N], U8, name="sv_scales", align_bytes=64)
+
+        turned = {}
+        grouped = {}
+
+        def unit_words(h, u):
+            if u < R * SU_PASSES:
+                r, g = divmod(u, SU_PASSES)
+                raw = su_raw[h][:, r, :].bitcast(F32)
+            else:
+                r, g = divmod(u - R * SU_PASSES, SV_PASSES)
+                raw = c_raw[h][:, r, :].bitcast(F32)
+            return raw, 256 * g
+
+        def turn(h, b):
+            bank = psum.tile([P, 4, P], F32, name="bank", tag="turn", bufs=8 - SUMB)
+            for i in range(4):
+                raw, w0 = unit_words(h, 2 * b + i // 2)
+                nc.tensor.transpose(bank[:, i, :], raw[:, w0 + i % 2 : w0 + 256 : 2], ident[:])
+            turned[h, b] = bank
+
+        def empty_turn(h, b, engine):
+            tile = stage.tile([P, 2, P, 4], BF16, name="row_grouped", align_bytes=64)
+            dst = tile[:].rearrange("p g m e -> p (g m e)").bitcast(F32)
+            dst = dst.rearrange("p (g m u) -> p g m u", g=2, u=2)
+            src = turned.pop((h, b))[:].rearrange("p (g u) m -> p g m u", g=2)
+            if engine == "v":
+                nc.vector.tensor_copy(out=dst, in_=src)
+            else:
+                nc.scalar.copy(out=dst, in_=src)
+            grouped[h, b] = tile
+
+        def quantize_rows(h, b):
+            u = slice(2 * b, 2 * b + 2)
+            nc.vector.quantize_mx(
+                out=row_codes[h][:, u, :].rearrange("p u m -> p (u m)").bitcast(E4M3X4),
+                scales=row_scales[h][:, u, :].rearrange("p u m -> p (u m)"),
+                in_=grouped.pop((h, b))[:].rearrange("p g m e -> p (g m e)"),
+            )
+
+        sv_grouped = {}
+
+        def interleave(g, n, engine, c0=0, c1=N_TILE):
+            if (g, n) not in sv_grouped:
+                sv_tile = stage.tile([P, N_TILE, 4], BF16, name="sv_tile", align_bytes=64)
+                sv_grouped[g, n] = sv_tile
+            dst = sv_grouped[g, n][:, c0:c1, :].rearrange("p (c i) t -> p c t i", i=4)
+            src = sv_raw[g, n][:, :, c0:c1].rearrange("p t (c i) -> p c t i", i=4)
+            if engine == "v":
+                nc.vector.tensor_copy(out=dst, in_=src)
+            else:
+                nc.scalar.copy(out=dst, in_=src)
+
+        def quantize_sv(g, n):
+            cols = slice(n * N_TILE, (n + 1) * N_TILE)
+            nc.vector.quantize_mx(
+                out=sv_codes[:, g, cols].bitcast(E4M3X4),
+                scales=sv_scales[:, g, cols],
+                in_=sv_grouped.pop((g, n))[:].rearrange("p c t -> p (c t)"),
+            )
+
+        acc = {}
+
+        def pass_d(h, r, n, g, start=False, stop=False):
+            if start:
+                if True:
+                    sum_bank = psum.tile([P, N_TILE], F32, name="sum_bank", tag="sum", bufs=SUMB)
+                acc[h, r, n] = sum_bank
+            u = r * SU_PASSES + g
+            nc.tensor.matmul_mx(
+                out=acc[h, r, n][:],
+                lhsT=row_codes[h][:, u, :].bitcast(E4M3X4),
+                lhsT_scale=row_scales[h][:, u, :],
+                rhs=words[:, g, 2 * n * N_TILE : 2 * (n + 1) * N_TILE].bitcast(E2M1X4),
+                rhs_scale=plane[:, g, n * N_TILE : (n + 1) * N_TILE],
+                start=start,
+                stop=stop,
+            )
+
+        def pass_sv(h, r, n, g, start=False, stop=False):
+            u = R * SU_PASSES + r * SV_PASSES + g
+            cols = slice(n * N_TILE, (n + 1) * N_TILE)
+            nc.tensor.matmul_mx(
+                out=acc[h, r, n][:],
+                lhsT=row_codes[h][:, u, :].bitcast(E4M3X4),
+                lhsT_scale=row_scales[h][:, u, :],
+                rhs=sv_codes[:, g, cols].bitcast(E4M3X4),
+                rhs_scale=sv_scales[:, g, cols],
+                start=start,
+                stop=stop,
+            )
+
+        tau = {}
+        work = {}
+
+        def col(n):
+            return slice(n * N_TILE, (n + 1) * N_TILE)
+
+        def take_sum(h, r, n):
+            if (h, r) not in tau:
+                tau_tile = stage.tile([P, N], F32, name="tau_tile")
+                work_tile = stage.tile([P, N], F32, name="work_tile")
+                tau[h, r] = tau_tile
+                work[h, r] = work_tile
+            nc.scalar.copy(out=tau[h, r][:, col(n)], in_=acc.pop((h, r, n))[:])
+
+        def subtract_u(h, r, n):
+            nc.vector.tensor_tensor(
+                out=work[h, r][:, col(n)], in0=tau[h, r][:, col(n)], in1=u_raw[h][:, r, col(n)], op=SUB
+            )
+
+        def exponent(h, r, n):
+            nc.scalar.activation(out=work[h, r][:, col(n)], in_=work[h, r][:, col(n)], func=EXP)
+
+        def closure(h, r, n):
+            nc.vector.scalar_tensor_tensor(
+                out=work[h, r][:, col(n)], in0=work[h, r][:, col(n)], scalar=1.0, in1=tau[h, r][:, col(n)], op0=SUB, op1=SUB
+            )
+
+        def store(dst, src, h, r, n0, n1):
+            cols = slice(n0 * N_TILE, n1 * N_TILE)
+            nc.sync.dma_start(out=dst[h][:, r, cols], in_=src[h, r][:, cols])
+
+        ev_count = [0]
+
+        def turn_items(bs):
+            for i in range(0, len(bs), 2):
+                pair = bs[i : i + 2]
+                for h, b in pair:
+                    turn(h, b)
+                for h, b in pair:
+                    empty_turn(h, b, EV[ev_count[0] % len(EV)])
+                    ev_count[0] += 1
+                for h, b in pair:
+                    quantize_rows(h, b)
+
+        prev = [None]
+        DONE_A = [0]
+
+        def finish(key):
+            h, r, n = key
+            exponent(h, r, n)
+            closure(h, r, n)
+            fine = key in FINE
+            if fine:
+                store(cnew_rows, work, h, r, n, n + 1)
+            elif n == 2:
+                store(cnew_rows, work, h, r, 0, 3)
+
+        def stage_end(key):
+            h, r, n = key
+            take_sum(h, r, n)
+            subtract_u(h, r, n)
+            fine = key in FINE
+            if fine:
+                store(tau_rows, tau, h, r, n, n + 1)
+            elif n == 2:
+                store(tau_rows, tau, h, r, 0, 3)
+            if prev[0] is not None:
+                finish(prev[0])
+            prev[0] = key
+
+        b_stages = [(0, r, n) for r in range(R) for n in range(N_TILES)]
+        if R0 == "n":
+            b_stages = [(0, r, n) for n in range(N_TILES) for r in range(R)]
+        b_stages += [(h, r, n) for h in range(1, GROUPS) for r in range(R) for n in range(N_TILES)]
+        FINE = b_stages[24 - NFINE :]
+        progress = {key: 0 for key in b_stages}
+
+        def advance(key, upto):
+            while progress[key] < upto:
+                i = progress[key]
+                if i < SU_PASSES:
+                    pass_d(*key, i, start=(i == 0))
+                else:
+                    pass_sv(*key, i - SU_PASSES, stop=(i == 4))
+                progress[key] = i + 1
+
+        for t in PROG:
+            k = int(t[1])
+            if t[0] == "s":
+                turn_items([(k, 0), (k, 1)])
+            if t[0] == "c":
+                turn_items([(k, 2), (k, 3), (k, 4)])
+            if t[0] == "v":
+                for n in range(N_TILES):
+                    m = V_IL[k][n]
+                    if m == "h":
+                        interleave(k, n, "v", 0, N_TILE // 2)
+                        interleave(k, n, "s", N_TILE // 2, N_TILE)
+                    else:
+                        interleave(k, n, m)
+                for n in range(N_TILES):
+                    quantize_sv(k, n)
+            if t[0] == "E":
+                for key in b_stages[:k]:
+                    advance(key, 2)
+            if t[0] == "F":
+                for key in b_stages[:k]:
+                    advance(key, 3)
+            if t[0] == "G":
+                for key in b_stages[:k]:
+                    advance(key, 4)
+        for key in b_stages:
+            advance(key, 5)
+            stage_end(key)
+        finish(prev[0])

@@ -35,6 +35,8 @@ def tile_rism_hnc_update_s1_kernel(tc, solute, d_words, d_scales, direct, solven
         stage = ctx.enter_context(tc.tile_pool(name="stage", bufs=4))
         psum = ctx.enter_context(tc.psum_pool(name="psum", bufs=1))
 
+        ctx.enter_context(tc.manual_schedule(engines={mybir.EngineType.PE}))
+
         ident = keep.tile([P, P], F32, name="ident")
         make_identity(nc, ident[:])
         plane = keep.tile([P, SU_PASSES, N], U8, name="plane", align_bytes=64)
@@ -86,13 +88,13 @@ def tile_rism_hnc_update_s1_kernel(tc, solute, d_words, d_scales, direct, solven
                     in_=d_scales.rearrange("g (q r) n -> r q g n", r=4)[r].bitcast(I32),
                 )
 
-        LOADS = "s0 v0 c0 d v1 s1 v2 c1 s2 u0 s3 c2 u1 c3 u2 u3".split()
-        PROG = "s0 v0 c0 E6 F6 v1 G6 s1 v2 c1 s2 s3 c2 c3".split()
+        LOADS = "s0 v0 c0 d v1 s1 v2 c1 u0 s2 c2 u1 s3 c3 u2 u3".split()
+        PROG = "v0 p00 p04 p02 E6 F6 v1 p10 G6 v2 p14 T0 p12 T1 T2 p20 T3 T4 T5 T6 T7 p22 T8 T9 T10 p24 T11 T12 p30 T13 T14 p32 T15 p34 T16 T17 T18 T19 T20 T21 T22 T23".split()
         BUFA = 6
         BUFB = 3
-        V_IL = ('svv', 'vvs', 'vsv')
+        V_IL = ('hvs', 'vsv', 'vsv')
         R0 = 'n'
-        NFINE = 3
+        NFINE = 9
         SUMB = 6
         EV = 's'
         load_d_scales()
@@ -295,11 +297,13 @@ def tile_rism_hnc_update_s1_kernel(tc, solute, d_words, d_scales, direct, solven
                 progress[key] = i + 1
 
         for t in PROG:
-            k = int(t[1])
-            if t[0] == "s":
-                turn_items([(k, 0), (k, 1)])
-            if t[0] == "c":
-                turn_items([(k, 2), (k, 3), (k, 4)])
+            k = int(t[1:])
+            if t[0] == "p":
+                h, b = divmod(k, 10)
+                turn_items([(h, x) for x in (b, b + 1) if x < BANKS])
+            if t[0] == "q":
+                h, b = divmod(k, 10)
+                turn_items([(h, b)])
             if t[0] == "v":
                 for n in range(N_TILES):
                     m = V_IL[k][n]
@@ -310,16 +314,10 @@ def tile_rism_hnc_update_s1_kernel(tc, solute, d_words, d_scales, direct, solven
                         interleave(k, n, m)
                 for n in range(N_TILES):
                     quantize_sv(k, n)
-            if t[0] == "E":
+            if t[0] in "EFG":
                 for key in b_stages[:k]:
-                    advance(key, 2)
-            if t[0] == "F":
-                for key in b_stages[:k]:
-                    advance(key, 3)
-            if t[0] == "G":
-                for key in b_stages[:k]:
-                    advance(key, 4)
-        for key in b_stages:
-            advance(key, 5)
-            stage_end(key)
+                    advance(key, 2 + "EFG".index(t[0]))
+            if t[0] == "T":
+                advance(b_stages[k], 5)
+                stage_end(b_stages[k])
         finish(prev[0])

@@ -35,7 +35,7 @@ def tile_rism_hnc_update_s1_kernel(tc, solute, d_words, d_scales, direct, solven
         stage = ctx.enter_context(tc.tile_pool(name="stage", bufs=4))
         psum = ctx.enter_context(tc.psum_pool(name="psum", bufs=1))
 
-        ctx.enter_context(tc.manual_schedule(engines={mybir.EngineType.PE}))
+        ctx.enter_context(tc.manual_schedule())
 
         ident = keep.tile([P, P], F32, name="ident")
         make_identity(nc, ident[:])
@@ -83,23 +83,24 @@ def tile_rism_hnc_update_s1_kernel(tc, solute, d_words, d_scales, direct, solven
 
         def load_d_scales():
             for r in range(4):
-                nc.scalar.dma_start(
+                nc.sync.dma_start(
                     out=plane[r:P:32, :, :].bitcast(I32),
                     in_=d_scales.rearrange("g (q r) n -> r q g n", r=4)[r].bitcast(I32),
                 )
 
-        LOADS = "s0 v0 c0 d v1 s1 v2 c1 u0 s2 c2 u1 s3 c3 u2 u3".split()
+        LOADS = "c0 x s0 v0 d v1 c1 v2 s1 s2 c2 u0 c3 u1 u2 u3 s3".split()
         PROG = "v0 p00 p04 p02 E6 F6 v1 p10 G6 v2 p14 T0 p12 T1 T2 p20 T3 T4 T5 T6 T7 p22 T8 T9 T10 p24 T11 T12 p30 T13 T14 p32 T15 p34 T16 T17 T18 T19 T20 T21 T22 T23".split()
         BUFA = 6
         BUFB = 3
         V_IL = ('hvs', 'vsv', 'vsv')
         R0 = 'n'
-        NFINE = 9
+        NFINE = 12
         SUMB = 6
-        EV = 's'
-        load_d_scales()
+        EV = "s"
         for it in LOADS:
             k = int(it[1]) if len(it) > 1 else 0
+            if it[0] == "x":
+                load_d_scales()
             if it[0] == "s":
                 load_su(k)
             if it[0] == "c":
@@ -140,7 +141,7 @@ def tile_rism_hnc_update_s1_kernel(tc, solute, d_words, d_scales, direct, solven
             turned[h, b] = bank
 
         def empty_turn(h, b, engine):
-            tile = stage.tile([P, 2, P, 4], BF16, name="row_grouped", align_bytes=64)
+            tile = stage.tile([P, 2, P, 4], BF16, name="row_grouped", align_bytes=64, bufs=6)
             dst = tile[:].rearrange("p g m e -> p (g m e)").bitcast(F32)
             dst = dst.rearrange("p (g m u) -> p g m u", g=2, u=2)
             src = turned.pop((h, b))[:].rearrange("p (g u) m -> p g m u", g=2)
@@ -216,69 +217,39 @@ def tile_rism_hnc_update_s1_kernel(tc, solute, d_words, d_scales, direct, solven
         def col(n):
             return slice(n * N_TILE, (n + 1) * N_TILE)
 
+        def parts(h, r, n):
+            step = N_TILE // 2 if (h, r, n) in SPLIT else N_TILE
+            return [slice(c, c + step) for c in range(n * N_TILE, (n + 1) * N_TILE, step)]
+
         def take_sum(h, r, n):
             if (h, r) not in tau:
                 tau_tile = stage.tile([P, N], F32, name="tau_tile")
                 work_tile = stage.tile([P, N], F32, name="work_tile")
                 tau[h, r] = tau_tile
                 work[h, r] = work_tile
-            nc.scalar.copy(out=tau[h, r][:, col(n)], in_=acc.pop((h, r, n))[:])
+            bank = acc.pop((h, r, n))
+            for c in parts(h, r, n):
+                nc.scalar.copy(out=tau[h, r][:, c], in_=bank[:, c.start - n * N_TILE : c.stop - n * N_TILE])
 
         def subtract_u(h, r, n):
-            nc.vector.tensor_tensor(
-                out=work[h, r][:, col(n)], in0=tau[h, r][:, col(n)], in1=u_raw[h][:, r, col(n)], op=SUB
-            )
+            for c in parts(h, r, n):
+                nc.vector.tensor_tensor(out=work[h, r][:, c], in0=tau[h, r][:, c], in1=u_raw[h][:, r, c], op=SUB)
 
         def exponent(h, r, n):
-            nc.scalar.activation(out=work[h, r][:, col(n)], in_=work[h, r][:, col(n)], func=EXP)
+            for c in parts(h, r, n):
+                nc.scalar.activation(out=work[h, r][:, c], in_=work[h, r][:, c], func=EXP)
 
         def closure(h, r, n):
-            nc.vector.scalar_tensor_tensor(
-                out=work[h, r][:, col(n)], in0=work[h, r][:, col(n)], scalar=1.0, in1=tau[h, r][:, col(n)], op0=SUB, op1=SUB
-            )
+            for c in parts(h, r, n):
+                nc.vector.scalar_tensor_tensor(
+                    out=work[h, r][:, c], in0=work[h, r][:, c], scalar=1.0, in1=tau[h, r][:, c], op0=SUB, op1=SUB
+                )
+
+        SPLIT = [(GROUPS - 1, R - 1, N_TILES - 1)]
 
         def store(dst, src, h, r, n0, n1):
             cols = slice(n0 * N_TILE, n1 * N_TILE)
             nc.sync.dma_start(out=dst[h][:, r, cols], in_=src[h, r][:, cols])
-
-        ev_count = [0]
-
-        def turn_items(bs):
-            for i in range(0, len(bs), 2):
-                pair = bs[i : i + 2]
-                for h, b in pair:
-                    turn(h, b)
-                for h, b in pair:
-                    empty_turn(h, b, EV[ev_count[0] % len(EV)])
-                    ev_count[0] += 1
-                for h, b in pair:
-                    quantize_rows(h, b)
-
-        prev = [None]
-        DONE_A = [0]
-
-        def finish(key):
-            h, r, n = key
-            exponent(h, r, n)
-            closure(h, r, n)
-            fine = key in FINE
-            if fine:
-                store(cnew_rows, work, h, r, n, n + 1)
-            elif n == 2:
-                store(cnew_rows, work, h, r, 0, 3)
-
-        def stage_end(key):
-            h, r, n = key
-            take_sum(h, r, n)
-            subtract_u(h, r, n)
-            fine = key in FINE
-            if fine:
-                store(tau_rows, tau, h, r, n, n + 1)
-            elif n == 2:
-                store(tau_rows, tau, h, r, 0, 3)
-            if prev[0] is not None:
-                finish(prev[0])
-            prev[0] = key
 
         b_stages = [(0, r, n) for r in range(R) for n in range(N_TILES)]
         if R0 == "n":
@@ -296,28 +267,74 @@ def tile_rism_hnc_update_s1_kernel(tc, solute, d_words, d_scales, direct, solven
                     pass_sv(*key, i - SU_PASSES, stop=(i == 4))
                 progress[key] = i + 1
 
-        for t in PROG:
-            k = int(t[1:])
-            if t[0] == "p":
-                h, b = divmod(k, 10)
-                turn_items([(h, x) for x in (b, b + 1) if x < BANKS])
-            if t[0] == "q":
-                h, b = divmod(k, 10)
-                turn_items([(h, b)])
-            if t[0] == "v":
-                for n in range(N_TILES):
-                    m = V_IL[k][n]
-                    if m == "h":
-                        interleave(k, n, "v", 0, N_TILE // 2)
-                        interleave(k, n, "s", N_TILE // 2, N_TILE)
-                    else:
-                        interleave(k, n, m)
-                for n in range(N_TILES):
-                    quantize_sv(k, n)
-            if t[0] in "EFG":
-                for key in b_stages[:k]:
+        def do_store(rows, tile, key):
+            h, r, n = key
+            if key in FINE:
+                store(rows, tile, h, r, n, n + 1)
+            elif n == N_TILES - 1:
+                store(rows, tile, h, r, 0, N_TILES)
+
+        LX, LB, LC = 3, 2, 4
+        SLOTS = {'p20': 2, 'p22': 10, 'p24': 6, 'p30': 16, 'p32': 12, 'p34': 18, 'p14': 6, 'p10': 0}
+        KL = 0
+        ORD = 'ebqxct'
+        EVD = 'p24 p30'
+        FRONT = "tp00 tp04 ep00 is00 kp00 fp04 tp02 iv02a kp04 iv01 is02b kv01 ep02 kv00 E6 kv02 is10 is12b kp02 iv12a tp12 iv11 kv11 ep12 kv10 F6 kv12 G6 iv20 is21 kv20 iv22 kv21 kv22 kp12".split()
+
+        def bank_list(t):
+            h, b = int(t[1]), int(t[2])
+            return [(h, x) for x in (b, b + 1) if x < BANKS]
+
+        for t in FRONT:
+            if t[1] == "p":
+                for hb in bank_list(t[1:]):
+                    if t[0] == "t":
+                        turn(*hb)
+                    if t[0] == "e":
+                        empty_turn(*hb, "s")
+                    if t[0] == "f":
+                        empty_turn(*hb, "v")
+                    if t[0] == "k":
+                        quantize_rows(*hb)
+            elif t[0] == "i":
+                half = t[4:]
+                lo = N_TILE // 2 if half == "b" else 0
+                hi = N_TILE // 2 if half == "a" else N_TILE
+                interleave(int(t[2]), int(t[3]), t[1], lo, hi)
+            elif t[0] == "k":
+                quantize_sv(int(t[2]), int(t[3]))
+            else:
+                for key in b_stages[: int(t[1])]:
                     advance(key, 2 + "EFG".index(t[0]))
-            if t[0] == "T":
-                advance(b_stages[k], 5)
-                stage_end(b_stages[k])
-        finish(prev[0])
+        slot = {}
+        for t, s in SLOTS.items():
+            slot.setdefault(s, []).append(t)
+        waiting = []
+        for s in range(len(b_stages) + LC + 1):
+            for t in slot.get(s, []):
+                for hb in bank_list(t):
+                    turn(*hb)
+            if s < len(b_stages):
+                advance(b_stages[s], 5)
+            due = [w for w in waiting if w[0] <= s]
+            waiting = [w for w in waiting if w[0] > s]
+            for o in ORD:
+                if o == "q":
+                    for w in due:
+                        for hb in bank_list(w[1]):
+                            quantize_rows(*hb)
+                if o == "e":
+                    for t in slot.get(s, []):
+                        for hb in bank_list(t):
+                            empty_turn(*hb, "v" if t in EVD.split() else "s")
+                        waiting.append((s + KL, t))
+                if o == "t" and s < len(b_stages):
+                    take_sum(*b_stages[s])
+                    do_store(tau_rows, tau, b_stages[s])
+                if o == "b" and LB <= s < len(b_stages) + LB:
+                    subtract_u(*b_stages[s - LB])
+                if o == "x" and LX <= s < len(b_stages) + LX:
+                    exponent(*b_stages[s - LX])
+                if o == "c" and LC <= s < len(b_stages) + LC:
+                    closure(*b_stages[s - LC])
+                    do_store(cnew_rows, work, b_stages[s - LC])

@@ -17,18 +17,49 @@ EXP = mybir.ActivationFunctionType.Exp
 SUB = mybir.AluOpType.subtract
 
 P = 128
-K_PASS = 512
+PACK = 4
+K_PASS = P * PACK
 SU_PASSES = M // K_PASS
 SV_PASSES = N // K_PASS
-R = 2
-GROUPS = M // (P * R)
+PASSES = SU_PASSES + SV_PASSES
 N_TILE = 512
 N_TILES = N // N_TILE
-UNITS = R * (SU_PASSES + SV_PASSES)
-BANKS = UNITS // 2
+
+R = 2
+GROUPS = M // (P * R)
+
+SU_UNITS = R * SU_PASSES
+UNITS = R * PASSES
+SU_BANKS = [0, 1]
+
+TURN_BANKS = 2
+SUM_BANKS = 6
+
+LAG = 5
+CATCH_UP = 10
+LAST_LAG = 2
+
+LATER = {
+    0: [(1, 0), (1, 1)],
+    2: [(2, 0), (2, 1)],
+    6: [(2, 2), (2, 3)],
+    9: [(2, 4), (3, 4)],
+    12: [(3, 0), (3, 1)],
+    14: [(3, 2), (3, 3)],
+}
+
+FIRST = [(0, r, n) for n in range(N_TILES) for r in range(R)]
+TILES = FIRST + [(h, r, n) for h in range(1, GROUPS) for r in range(R) for n in range(N_TILES)]
+SINGLE_STORES = TILES[len(TILES) // 2 :]
 
 
-def tile_rism_hnc_update_s1_kernel(tc, solute, d_words, d_scales, direct, solvent, potential, tau_out, c_out):
+def columns(n):
+    return slice(n * N_TILE, (n + 1) * N_TILE)
+
+
+def tile_rism_hnc_update_s1_kernel(
+    tc, solute, d_words, d_scales, direct, solvent, potential, tau_out, c_out
+):
     nc = tc.nc
     with ExitStack() as ctx:
         keep = ctx.enter_context(tc.tile_pool(name="keep", bufs=1))
@@ -39,8 +70,9 @@ def tile_rism_hnc_update_s1_kernel(tc, solute, d_words, d_scales, direct, solven
 
         ident = keep.tile([P, P], F32, name="ident")
         make_identity(nc, ident[:])
-        plane = keep.tile([P, SU_PASSES, N], U8, name="plane", align_bytes=64)
-        nc.vector.memset(plane[:].rearrange("p g n -> p (g n)").bitcast(I32), 0)
+
+        d_plane = keep.tile([P, SU_PASSES, N], U8, name="d_plane", align_bytes=64)
+        nc.vector.memset(d_plane[:].rearrange("p g n -> p (g n)").bitcast(I32), 0)
         warm = keep.tile([P, 1], F32, name="warm")
         nc.vector.memset(warm[:], 0.0)
 
@@ -48,14 +80,11 @@ def tile_rism_hnc_update_s1_kernel(tc, solute, d_words, d_scales, direct, solven
         c_rows = direct.rearrange("(h p r) k -> h p r k", p=P, r=R)
         u_rows = potential.rearrange("(h p r) n -> h p r n", p=P, r=R)
         tau_rows = tau_out.rearrange("(h p r) n -> h p r n", p=P, r=R)
-        cnew_rows = c_out.rearrange("(h p r) n -> h p r n", p=P, r=R)
-        sv_rows = solvent.rearrange("(g p j) n -> g p j n", p=P, j=4)
+        c_new_rows = c_out.rearrange("(h p r) n -> h p r n", p=P, r=R)
+        sv_rows = solvent.rearrange("(g p t) n -> g p t n", p=P, t=PACK)
 
-        su_raw = {}
-        c_raw = {}
-        u_raw = {}
-        sv_raw = {}
-        words = keep.tile([P, SU_PASSES, 2 * N], U8, name="words", align_bytes=64)
+        su_raw, c_raw, u_raw, sv_raw = {}, {}, {}, {}
+        d_codes = keep.tile([P, SU_PASSES, 2 * N], U8, name="d_codes", align_bytes=64)
 
         def load_su(h):
             su_raw[h] = keep.tile([P, R, M], BF16, name=f"su_raw{h}")
@@ -69,272 +98,245 @@ def tile_rism_hnc_update_s1_kernel(tc, solute, d_words, d_scales, direct, solven
             u_raw[h] = keep.tile([P, R, N], BF16, name=f"u_raw{h}")
             nc.sync.dma_start(out=u_raw[h][:], in_=u_rows[h])
 
-        def load_sv(g, n0, n1):
-            cols = slice(n0 * N_TILE, n1 * N_TILE)
-            tile = keep.tile([P, 4, (n1 - n0) * N_TILE], BF16, name=f"sv_raw{g}_{n0}")
-            nc.sync.dma_start(out=tile[:], in_=sv_rows[g][:, :, cols])
-            for n in range(n0, n1):
-                sv_raw[g, n] = tile[:, :, (n - n0) * N_TILE : (n + 1 - n0) * N_TILE]
+        def load_sv(g):
+            sv_raw[g] = keep.tile([P, PACK, N], BF16, name=f"sv_raw{g}")
+            nc.sync.dma_start(out=sv_raw[g][:], in_=sv_rows[g])
 
-        def load_d():
-            nc.sync.dma_start(
-                out=words[:].bitcast(I32), in_=d_words.rearrange("g p b -> p g b").bitcast(I32)
-            )
+        def load_d_codes():
+            nc.sync.dma_start(out=d_codes[:].bitcast(I32), in_=d_words.rearrange("g p b -> p g b").bitcast(I32))
 
         def load_d_scales():
-            for r in range(4):
+            for i in range(4):
                 nc.sync.dma_start(
-                    out=plane[r:P:32, :, :].bitcast(I32),
-                    in_=d_scales.rearrange("g (q r) n -> r q g n", r=4)[r].bitcast(I32),
+                    out=d_plane[i:P:32, :, :].bitcast(I32),
+                    in_=d_scales.rearrange("g (q i) n -> i q g n", i=4)[i].bitcast(I32),
                 )
 
-        LOADS = "c0 x s0 v0 d v1 c1 v2 s1 s2 c2 u0 c3 u1 u2 u3 s3".split()
-        PROG = "v0 p00 p04 p02 E6 F6 v1 p10 G6 v2 p14 T0 p12 T1 T2 p20 T3 T4 T5 T6 T7 p22 T8 T9 T10 p24 T11 T12 p30 T13 T14 p32 T15 p34 T16 T17 T18 T19 T20 T21 T22 T23".split()
-        BUFA = 6
-        BUFB = 3
-        V_IL = ('hvs', 'vsv', 'vsv')
-        R0 = 'n'
-        NFINE = 12
-        SUMB = 6
-        EV = "s"
-        for it in LOADS:
-            k = int(it[1]) if len(it) > 1 else 0
-            if it[0] == "x":
-                load_d_scales()
-            if it[0] == "s":
-                load_su(k)
-            if it[0] == "c":
-                load_c(k)
-            if it[0] == "u":
-                load_u(k)
-            if it[0] == "v":
-                load_sv(k, 0, 3)
-            if it[0] == "d":
-                load_d()
+        load_su(0)
+        load_c(0)
+        load_d_scales()
+        load_sv(0)
+        load_d_codes()
+        load_sv(1)
+        load_c(1)
+        load_sv(2)
+        load_su(1)
+        load_su(2)
+        load_u(0)
+        load_c(2)
+        load_c(3)
+        load_u(1)
+        load_u(2)
+        load_su(3)
+        load_u(3)
+
         nc.scalar.activation(out=warm[:], in_=warm[:], func=EXP)
 
-        row_codes = {}
-        row_scales = {}
+        row_codes, row_scales = {}, {}
         for h in range(GROUPS):
             row_codes[h] = keep.tile([P, UNITS, P], U32, name=f"row_codes{h}", align_bytes=64)
             row_scales[h] = keep.tile([P, UNITS, P], U8, name=f"row_scales{h}", align_bytes=64)
         sv_codes = keep.tile([P, SV_PASSES, N], U32, name="sv_codes", align_bytes=64)
         sv_scales = keep.tile([P, SV_PASSES, N], U8, name="sv_scales", align_bytes=64)
 
-        turned = {}
-        grouped = {}
-
-        def unit_words(h, u):
-            if u < R * SU_PASSES:
-                r, g = divmod(u, SU_PASSES)
-                raw = su_raw[h][:, r, :].bitcast(F32)
-            else:
-                r, g = divmod(u - R * SU_PASSES, SV_PASSES)
-                raw = c_raw[h][:, r, :].bitcast(F32)
-            return raw, 256 * g
+        turned, row_grouped, sv_grouped = {}, {}, {}
 
         def turn(h, b):
-            bank = psum.tile([P, 4, P], F32, name="bank", tag="turn", bufs=8 - SUMB)
-            for i in range(4):
-                raw, w0 = unit_words(h, 2 * b + i // 2)
-                nc.tensor.transpose(bank[:, i, :], raw[:, w0 + i % 2 : w0 + 256 : 2], ident[:])
+            bank = psum.tile([P, 4, P], F32, name="bank", tag="turn", bufs=TURN_BANKS)
+            for j in range(2):
+                unit = 2 * b + j
+                if unit < SU_UNITS:
+                    r, g = divmod(unit, SU_PASSES)
+                    raw = su_raw[h]
+                else:
+                    r, g = divmod(unit - SU_UNITS, SV_PASSES)
+                    raw = c_raw[h]
+                words = raw[:, r, :].bitcast(F32)
+                for i in range(2):
+                    nc.tensor.transpose(bank[:, 2 * j + i, :], words[:, 256 * g + i : 256 * (g + 1) : 2], ident[:])
             turned[h, b] = bank
 
-        def empty_turn(h, b, engine):
-            tile = stage.tile([P, 2, P, 4], BF16, name="row_grouped", align_bytes=64, bufs=6)
-            dst = tile[:].rearrange("p g m e -> p (g m e)").bitcast(F32)
-            dst = dst.rearrange("p (g m u) -> p g m u", g=2, u=2)
-            src = turned.pop((h, b))[:].rearrange("p (g u) m -> p g m u", g=2)
-            if engine == "v":
-                nc.vector.tensor_copy(out=dst, in_=src)
-            else:
-                nc.scalar.copy(out=dst, in_=src)
-            grouped[h, b] = tile
+        def empty_turned(h, b, copy):
+            grouped = stage.tile([P, 2, P, PACK], BF16, name="row_tile", align_bytes=64, bufs=6)
+            dst = grouped[:].rearrange("p j m t -> p (j m t)").bitcast(F32)
+            copy(
+                out=dst.rearrange("p (j m i) -> p j m i", j=2, i=2),
+                in_=turned.pop((h, b))[:].rearrange("p (j i) m -> p j m i", j=2),
+            )
+            row_grouped[h, b] = grouped
 
         def quantize_rows(h, b):
-            u = slice(2 * b, 2 * b + 2)
+            units = slice(2 * b, 2 * b + 2)
             nc.vector.quantize_mx(
-                out=row_codes[h][:, u, :].rearrange("p u m -> p (u m)").bitcast(E4M3X4),
-                scales=row_scales[h][:, u, :].rearrange("p u m -> p (u m)"),
-                in_=grouped.pop((h, b))[:].rearrange("p g m e -> p (g m e)"),
+                out=row_codes[h][:, units, :].rearrange("p u m -> p (u m)").bitcast(E4M3X4),
+                scales=row_scales[h][:, units, :].rearrange("p u m -> p (u m)"),
+                in_=row_grouped.pop((h, b))[:].rearrange("p j m t -> p (j m t)"),
             )
 
-        sv_grouped = {}
-
-        def interleave(g, n, engine, c0=0, c1=N_TILE):
+        def interleave(g, n, copy, c0=0, c1=N_TILE):
             if (g, n) not in sv_grouped:
-                sv_tile = stage.tile([P, N_TILE, 4], BF16, name="sv_tile", align_bytes=64)
+                sv_tile = stage.tile([P, N_TILE, PACK], BF16, name="sv_tile", align_bytes=64)
                 sv_grouped[g, n] = sv_tile
-            dst = sv_grouped[g, n][:, c0:c1, :].rearrange("p (c i) t -> p c t i", i=4)
-            src = sv_raw[g, n][:, :, c0:c1].rearrange("p t (c i) -> p c t i", i=4)
-            if engine == "v":
-                nc.vector.tensor_copy(out=dst, in_=src)
-            else:
-                nc.scalar.copy(out=dst, in_=src)
+            copy(
+                out=sv_grouped[g, n][:, c0:c1, :].rearrange("p (c i) t -> p c t i", i=4),
+                in_=sv_raw[g][:, :, n * N_TILE + c0 : n * N_TILE + c1].rearrange("p t (c i) -> p c t i", i=4),
+            )
 
         def quantize_sv(g, n):
-            cols = slice(n * N_TILE, (n + 1) * N_TILE)
             nc.vector.quantize_mx(
-                out=sv_codes[:, g, cols].bitcast(E4M3X4),
-                scales=sv_scales[:, g, cols],
+                out=sv_codes[:, g, columns(n)].bitcast(E4M3X4),
+                scales=sv_scales[:, g, columns(n)],
                 in_=sv_grouped.pop((g, n))[:].rearrange("p c t -> p (c t)"),
             )
 
-        acc = {}
+        sums = {}
+        passes_done = {key: 0 for key in TILES}
 
-        def pass_d(h, r, n, g, start=False, stop=False):
-            if start:
-                if True:
-                    sum_bank = psum.tile([P, N_TILE], F32, name="sum_bank", tag="sum", bufs=SUMB)
-                acc[h, r, n] = sum_bank
-            u = r * SU_PASSES + g
-            nc.tensor.matmul_mx(
-                out=acc[h, r, n][:],
-                lhsT=row_codes[h][:, u, :].bitcast(E4M3X4),
-                lhsT_scale=row_scales[h][:, u, :],
-                rhs=words[:, g, 2 * n * N_TILE : 2 * (n + 1) * N_TILE].bitcast(E2M1X4),
-                rhs_scale=plane[:, g, n * N_TILE : (n + 1) * N_TILE],
-                start=start,
-                stop=stop,
-            )
+        def multiply(key, upto):
+            h, r, n = key
+            for k in range(passes_done[key], upto):
+                if k == 0:
+                    sum_bank = psum.tile([P, N_TILE], F32, name="sum_bank", tag="sum", bufs=SUM_BANKS)
+                    sums[key] = sum_bank
+                if k < SU_PASSES:
+                    unit = r * SU_PASSES + k
+                    rhs = d_codes[:, k, 2 * n * N_TILE : 2 * (n + 1) * N_TILE].bitcast(E2M1X4)
+                    rhs_scale = d_plane[:, k, columns(n)]
+                else:
+                    g = k - SU_PASSES
+                    unit = SU_UNITS + r * SV_PASSES + g
+                    rhs = sv_codes[:, g, columns(n)].bitcast(E4M3X4)
+                    rhs_scale = sv_scales[:, g, columns(n)]
+                nc.tensor.matmul_mx(
+                    out=sums[key][:],
+                    lhsT=row_codes[h][:, unit, :].bitcast(E4M3X4),
+                    lhsT_scale=row_scales[h][:, unit, :],
+                    rhs=rhs,
+                    rhs_scale=rhs_scale,
+                    start=(k == 0),
+                    stop=(k == PASSES - 1),
+                )
+            passes_done[key] = upto
 
-        def pass_sv(h, r, n, g, start=False, stop=False):
-            u = R * SU_PASSES + r * SV_PASSES + g
-            cols = slice(n * N_TILE, (n + 1) * N_TILE)
-            nc.tensor.matmul_mx(
-                out=acc[h, r, n][:],
-                lhsT=row_codes[h][:, u, :].bitcast(E4M3X4),
-                lhsT_scale=row_scales[h][:, u, :],
-                rhs=sv_codes[:, g, cols].bitcast(E4M3X4),
-                rhs_scale=sv_scales[:, g, cols],
-                start=start,
-                stop=stop,
-            )
+        tau, work = {}, {}
 
-        tau = {}
-        work = {}
+        def pieces(key):
+            step = N_TILE // 2 if key == TILES[-1] else N_TILE
+            n0 = key[2] * N_TILE
+            return [slice(c, c + step) for c in range(n0, n0 + N_TILE, step)]
 
-        def col(n):
-            return slice(n * N_TILE, (n + 1) * N_TILE)
+        def store(rows, tiles, key):
+            h, r, n = key
+            if key in SINGLE_STORES:
+                nc.sync.dma_start(out=rows[h][:, r, columns(n)], in_=tiles[h, r][:, columns(n)])
+            elif n == N_TILES - 1:
+                nc.sync.dma_start(out=rows[h][:, r, :], in_=tiles[h, r][:])
 
-        def parts(h, r, n):
-            step = N_TILE // 2 if (h, r, n) in SPLIT else N_TILE
-            return [slice(c, c + step) for c in range(n * N_TILE, (n + 1) * N_TILE, step)]
-
-        def take_sum(h, r, n):
+        def take_sum(key):
+            h, r, n = key
             if (h, r) not in tau:
                 tau_tile = stage.tile([P, N], F32, name="tau_tile")
                 work_tile = stage.tile([P, N], F32, name="work_tile")
                 tau[h, r] = tau_tile
                 work[h, r] = work_tile
-            bank = acc.pop((h, r, n))
-            for c in parts(h, r, n):
-                nc.scalar.copy(out=tau[h, r][:, c], in_=bank[:, c.start - n * N_TILE : c.stop - n * N_TILE])
+            bank = sums.pop(key)
+            n0 = n * N_TILE
+            for c in pieces(key):
+                nc.scalar.copy(out=tau[h, r][:, c], in_=bank[:, c.start - n0 : c.stop - n0])
+            store(tau_rows, tau, key)
 
-        def subtract_u(h, r, n):
-            for c in parts(h, r, n):
+        def subtract_u(key):
+            h, r, n = key
+            for c in pieces(key):
                 nc.vector.tensor_tensor(out=work[h, r][:, c], in0=tau[h, r][:, c], in1=u_raw[h][:, r, c], op=SUB)
 
-        def exponent(h, r, n):
-            for c in parts(h, r, n):
+        def exponentiate(key):
+            h, r, n = key
+            for c in pieces(key):
                 nc.scalar.activation(out=work[h, r][:, c], in_=work[h, r][:, c], func=EXP)
 
-        def closure(h, r, n):
-            for c in parts(h, r, n):
+        def close(key):
+            h, r, n = key
+            for c in pieces(key):
                 nc.vector.scalar_tensor_tensor(
                     out=work[h, r][:, c], in0=work[h, r][:, c], scalar=1.0, in1=tau[h, r][:, c], op0=SUB, op1=SUB
                 )
+            store(c_new_rows, work, key)
 
-        SPLIT = [(GROUPS - 1, R - 1, N_TILES - 1)]
+        vector_copy = nc.vector.tensor_copy
+        scalar_copy = nc.scalar.copy
+        half = N_TILE // 2
 
-        def store(dst, src, h, r, n0, n1):
-            cols = slice(n0 * N_TILE, n1 * N_TILE)
-            nc.sync.dma_start(out=dst[h][:, r, cols], in_=src[h, r][:, cols])
+        for b in SU_BANKS:
+            turn(0, b)
+        for b in SU_BANKS:
+            empty_turned(0, b, vector_copy)
+        for b in SU_BANKS:
+            quantize_rows(0, b)
+        interleave(0, 1, vector_copy)
+        turn(0, 2)
+        turn(0, 3)
+        interleave(0, 2, vector_copy, 0, half)
+        empty_turned(0, 2, scalar_copy)
+        empty_turned(0, 3, scalar_copy)
+        interleave(0, 0, scalar_copy)
+        quantize_sv(0, 1)
+        quantize_rows(0, 2)
+        quantize_rows(0, 3)
+        interleave(0, 2, scalar_copy, half, N_TILE)
+        turn(0, 4)
+        for key in FIRST:
+            multiply(key, SU_PASSES)
+        empty_turned(0, 4, scalar_copy)
+        quantize_sv(0, 0)
+        interleave(1, 0, scalar_copy)
+        for key in FIRST[:2]:
+            multiply(key, SU_PASSES + 1)
+        turn(1, 2)
+        turn(1, 3)
+        quantize_sv(0, 2)
+        for key in FIRST[2:4]:
+            multiply(key, SU_PASSES + 1)
+        quantize_rows(0, 4)
+        turn(1, 4)
+        empty_turned(1, 2, scalar_copy)
+        empty_turned(1, 3, scalar_copy)
+        interleave(1, 1, vector_copy)
+        empty_turned(1, 4, scalar_copy)
+        interleave(1, 2, vector_copy)
+        interleave(2, 1, scalar_copy)
+        for n in range(N_TILES):
+            quantize_sv(1, n)
+        interleave(2, 0, vector_copy)
+        quantize_sv(2, 0)
+        for key in FIRST:
+            multiply(key, PASSES - 1)
+        interleave(2, 2, vector_copy)
+        quantize_sv(2, 1)
+        quantize_sv(2, 2)
+        for b in (2, 3, 4):
+            quantize_rows(1, b)
 
-        b_stages = [(0, r, n) for r in range(R) for n in range(N_TILES)]
-        if R0 == "n":
-            b_stages = [(0, r, n) for n in range(N_TILES) for r in range(R)]
-        b_stages += [(h, r, n) for h in range(1, GROUPS) for r in range(R) for n in range(N_TILES)]
-        FINE = b_stages[24 - NFINE :]
-        progress = {key: 0 for key in b_stages}
-
-        def advance(key, upto):
-            while progress[key] < upto:
-                i = progress[key]
-                if i < SU_PASSES:
-                    pass_d(*key, i, start=(i == 0))
-                else:
-                    pass_sv(*key, i - SU_PASSES, stop=(i == 4))
-                progress[key] = i + 1
-
-        def do_store(rows, tile, key):
-            h, r, n = key
-            if key in FINE:
-                store(rows, tile, h, r, n, n + 1)
-            elif n == N_TILES - 1:
-                store(rows, tile, h, r, 0, N_TILES)
-
-        LX, LB, LC = 3, 2, 4
-        SLOTS = {'p20': 2, 'p22': 10, 'p24': 6, 'p30': 16, 'p32': 12, 'p34': 18, 'p14': 6, 'p10': 0}
-        KL = 0
-        ORD = 'ebqxct'
-        EVD = 'p24 p30'
-        FRONT = "tp00 tp04 ep00 is00 kp00 fp04 tp02 iv02a kp04 iv01 is02b kv01 ep02 kv00 E6 kv02 is10 is12b kp02 iv12a tp12 iv11 kv11 ep12 kv10 F6 kv12 G6 iv20 is21 kv20 iv22 kv21 kv22 kp12".split()
-
-        def bank_list(t):
-            h, b = int(t[1]), int(t[2])
-            return [(h, x) for x in (b, b + 1) if x < BANKS]
-
-        for t in FRONT:
-            if t[1] == "p":
-                for hb in bank_list(t[1:]):
-                    if t[0] == "t":
-                        turn(*hb)
-                    if t[0] == "e":
-                        empty_turn(*hb, "s")
-                    if t[0] == "f":
-                        empty_turn(*hb, "v")
-                    if t[0] == "k":
-                        quantize_rows(*hb)
-            elif t[0] == "i":
-                half = t[4:]
-                lo = N_TILE // 2 if half == "b" else 0
-                hi = N_TILE // 2 if half == "a" else N_TILE
-                interleave(int(t[2]), int(t[3]), t[1], lo, hi)
-            elif t[0] == "k":
-                quantize_sv(int(t[2]), int(t[3]))
-            else:
-                for key in b_stages[: int(t[1])]:
-                    advance(key, 2 + "EFG".index(t[0]))
-        slot = {}
-        for t, s in SLOTS.items():
-            slot.setdefault(s, []).append(t)
-        waiting = []
-        for s in range(len(b_stages) + LC + 1):
-            for t in slot.get(s, []):
-                for hb in bank_list(t):
-                    turn(*hb)
-            if s < len(b_stages):
-                advance(b_stages[s], 5)
-            due = [w for w in waiting if w[0] <= s]
-            waiting = [w for w in waiting if w[0] > s]
-            for o in ORD:
-                if o == "q":
-                    for w in due:
-                        for hb in bank_list(w[1]):
-                            quantize_rows(*hb)
-                if o == "e":
-                    for t in slot.get(s, []):
-                        for hb in bank_list(t):
-                            empty_turn(*hb, "v" if t in EVD.split() else "s")
-                        waiting.append((s + KL, t))
-                if o == "t" and s < len(b_stages):
-                    take_sum(*b_stages[s])
-                    do_store(tau_rows, tau, b_stages[s])
-                if o == "b" and LB <= s < len(b_stages) + LB:
-                    subtract_u(*b_stages[s - LB])
-                if o == "x" and LX <= s < len(b_stages) + LX:
-                    exponent(*b_stages[s - LX])
-                if o == "c" and LC <= s < len(b_stages) + LC:
-                    closure(*b_stages[s - LC])
-                    do_store(cnew_rows, work, b_stages[s - LC])
+        exp_done, close_done = 0, 0
+        for s in range(len(TILES) + LAST_LAG):
+            later = LATER.get(s, [])
+            for h, b in later:
+                turn(h, b)
+            if s < len(TILES):
+                multiply(TILES[s], PASSES)
+            for h, b in later:
+                empty_turned(h, b, scalar_copy)
+            lag = max(LAST_LAG, LAG - max(0, s - CATCH_UP))
+            ready = max(0, min(len(TILES), s - lag + 1))
+            for key in TILES[exp_done:ready]:
+                exponentiate(key)
+            exp_done = ready
+            if 1 <= s <= len(TILES):
+                subtract_u(TILES[s - 1])
+            for h, b in later:
+                quantize_rows(h, b)
+            for key in TILES[close_done:ready]:
+                close(key)
+            close_done = ready
+            if s < len(TILES):
+                take_sum(TILES[s])

from contextlib import ExitStack

import concourse.mybir as mybir
from concourse.masks import make_identity

M, N = 1024, 1536
FLOPS = 2 * M * N * (M + N)

F32 = mybir.dt.float32
BF16 = mybir.dt.bfloat16
I32 = mybir.dt.int32
U32 = mybir.dt.uint32
U8 = mybir.dt.uint8
E4M3X4 = mybir.dt.float8_e4m3fn_x4
E2M1X4 = mybir.dt.float4_e2m1fn_x4
EXP = mybir.ActivationFunctionType.Exp
SUB = mybir.AluOpType.subtract

P = 128
PACK = 4
K_PASS = P * PACK
SU_PASSES = M // K_PASS
SV_PASSES = N // K_PASS
PASSES = SU_PASSES + SV_PASSES
N_TILE = 512
N_TILES = N // N_TILE

R = 2
GROUPS = M // (P * R)

SU_UNITS = R * SU_PASSES
UNITS = R * PASSES
SU_BANKS = [0, 1]

TURN_BANKS = 2
SUM_BANKS = 6

LAG = 5
CATCH_UP = 10
LAST_LAG = 2

LATER = {
    0: [(1, 0), (1, 1)],
    2: [(2, 0), (2, 1)],
    6: [(2, 2), (2, 3)],
    9: [(2, 4), (3, 4)],
    12: [(3, 0), (3, 1)],
    14: [(3, 2), (3, 3)],
}

FIRST = [(0, r, n) for n in range(N_TILES) for r in range(R)]
TILES = FIRST + [(h, r, n) for h in range(1, GROUPS) for r in range(R) for n in range(N_TILES)]
SINGLE_STORES = TILES[len(TILES) // 2 :]


def columns(n):
    return slice(n * N_TILE, (n + 1) * N_TILE)


def tile_rism_hnc_update_s1_kernel(
    tc, solute, d_words, d_scales, direct, solvent, potential, tau_out, c_out
):
    nc = tc.nc
    with ExitStack() as ctx:
        keep = ctx.enter_context(tc.tile_pool(name="keep", bufs=1))
        stage = ctx.enter_context(tc.tile_pool(name="stage", bufs=4))
        psum = ctx.enter_context(tc.psum_pool(name="psum", bufs=1))

        ctx.enter_context(tc.manual_schedule())

        ident = keep.tile([P, P], F32, name="ident")
        make_identity(nc, ident[:])

        d_plane = keep.tile([P, SU_PASSES, N], U8, name="d_plane", align_bytes=64)
        nc.vector.memset(d_plane[:].rearrange("p g n -> p (g n)").bitcast(I32), 0)
        warm = keep.tile([P, 1], F32, name="warm")
        nc.vector.memset(warm[:], 0.0)

        su_rows = solute.rearrange("(h p r) k -> h p r k", p=P, r=R)
        c_rows = direct.rearrange("(h p r) k -> h p r k", p=P, r=R)
        u_rows = potential.rearrange("(h p r) n -> h p r n", p=P, r=R)
        tau_rows = tau_out.rearrange("(h p r) n -> h p r n", p=P, r=R)
        c_new_rows = c_out.rearrange("(h p r) n -> h p r n", p=P, r=R)
        sv_rows = solvent.rearrange("(g p t) n -> g p t n", p=P, t=PACK)

        su_raw, c_raw, u_raw, sv_raw = {}, {}, {}, {}
        d_codes = keep.tile([P, SU_PASSES, 2 * N], U8, name="d_codes", align_bytes=64)

        def load_su(h):
            su_raw[h] = keep.tile([P, R, M], BF16, name=f"su_raw{h}")
            nc.sync.dma_start(out=su_raw[h][:], in_=su_rows[h])

        def load_c(h):
            c_raw[h] = keep.tile([P, R, N], BF16, name=f"c_raw{h}")
            nc.sync.dma_start(out=c_raw[h][:], in_=c_rows[h])

        def load_u(h):
            u_raw[h] = keep.tile([P, R, N], BF16, name=f"u_raw{h}")
            nc.sync.dma_start(out=u_raw[h][:], in_=u_rows[h])

        def load_sv(g):
            sv_raw[g] = keep.tile([P, PACK, N], BF16, name=f"sv_raw{g}")
            nc.sync.dma_start(out=sv_raw[g][:], in_=sv_rows[g])

        def load_d_codes():
            nc.sync.dma_start(out=d_codes[:].bitcast(I32), in_=d_words.rearrange("g p b -> p g b").bitcast(I32))

        def load_d_scales():
            for i in range(4):
                nc.sync.dma_start(
                    out=d_plane[i:P:32, :, :].bitcast(I32),
                    in_=d_scales.rearrange("g (q i) n -> i q g n", i=4)[i].bitcast(I32),
                )

        load_su(0)
        load_c(0)
        load_d_scales()
        load_sv(0)
        load_d_codes()
        load_sv(1)
        load_c(1)
        load_sv(2)
        load_su(1)
        load_su(2)
        load_u(0)
        load_c(2)
        load_c(3)
        load_u(1)
        load_u(2)
        load_su(3)
        load_u(3)

        nc.scalar.activation(out=warm[:], in_=warm[:], func=EXP)

        row_codes, row_scales = {}, {}
        for h in range(GROUPS):
            row_codes[h] = keep.tile([P, UNITS, P], U32, name=f"row_codes{h}", align_bytes=64)
            row_scales[h] = keep.tile([P, UNITS, P], U8, name=f"row_scales{h}", align_bytes=64)
        sv_codes = keep.tile([P, SV_PASSES, N], U32, name="sv_codes", align_bytes=64)
        sv_scales = keep.tile([P, SV_PASSES, N], U8, name="sv_scales", align_bytes=64)

        turned, row_grouped, sv_grouped = {}, {}, {}

        def turn(h, b):
            bank = psum.tile([P, 4, P], F32, name="bank", tag="turn", bufs=TURN_BANKS)
            for j in range(2):
                unit = 2 * b + j
                if unit < SU_UNITS:
                    r, g = divmod(unit, SU_PASSES)
                    raw = su_raw[h]
                else:
                    r, g = divmod(unit - SU_UNITS, SV_PASSES)
                    raw = c_raw[h]
                words = raw[:, r, :].bitcast(F32)
                for i in range(2):
                    nc.tensor.transpose(bank[:, 2 * j + i, :], words[:, 256 * g + i : 256 * (g + 1) : 2], ident[:])
            turned[h, b] = bank

        def empty_turned(h, b, copy):
            grouped = stage.tile([P, 2, P, PACK], BF16, name="row_tile", align_bytes=64, bufs=6)
            dst = grouped[:].rearrange("p j m t -> p (j m t)").bitcast(F32)
            copy(
                out=dst.rearrange("p (j m i) -> p j m i", j=2, i=2),
                in_=turned.pop((h, b))[:].rearrange("p (j i) m -> p j m i", j=2),
            )
            row_grouped[h, b] = grouped

        def quantize_rows(h, b):
            units = slice(2 * b, 2 * b + 2)
            nc.vector.quantize_mx(
                out=row_codes[h][:, units, :].rearrange("p u m -> p (u m)").bitcast(E4M3X4),
                scales=row_scales[h][:, units, :].rearrange("p u m -> p (u m)"),
                in_=row_grouped.pop((h, b))[:].rearrange("p j m t -> p (j m t)"),
            )

        def interleave(g, n, copy, c0=0, c1=N_TILE):
            if (g, n) not in sv_grouped:
                sv_tile = stage.tile([P, N_TILE, PACK], BF16, name="sv_tile", align_bytes=64)
                sv_grouped[g, n] = sv_tile
            copy(
                out=sv_grouped[g, n][:, c0:c1, :].rearrange("p (c i) t -> p c t i", i=4),
                in_=sv_raw[g][:, :, n * N_TILE + c0 : n * N_TILE + c1].rearrange("p t (c i) -> p c t i", i=4),
            )

        def quantize_sv(g, n):
            nc.vector.quantize_mx(
                out=sv_codes[:, g, columns(n)].bitcast(E4M3X4),
                scales=sv_scales[:, g, columns(n)],
                in_=sv_grouped.pop((g, n))[:].rearrange("p c t -> p (c t)"),
            )

        sums = {}
        passes_done = {key: 0 for key in TILES}

        def multiply(key, upto):
            h, r, n = key
            for k in range(passes_done[key], upto):
                if k == 0:
                    sum_bank = psum.tile([P, N_TILE], F32, name="sum_bank", tag="sum", bufs=SUM_BANKS)
                    sums[key] = sum_bank
                if k < SU_PASSES:
                    unit = r * SU_PASSES + k
                    rhs = d_codes[:, k, 2 * n * N_TILE : 2 * (n + 1) * N_TILE].bitcast(E2M1X4)
                    rhs_scale = d_plane[:, k, columns(n)]
                else:
                    g = k - SU_PASSES
                    unit = SU_UNITS + r * SV_PASSES + g
                    rhs = sv_codes[:, g, columns(n)].bitcast(E4M3X4)
                    rhs_scale = sv_scales[:, g, columns(n)]
                nc.tensor.matmul_mx(
                    out=sums[key][:],
                    lhsT=row_codes[h][:, unit, :].bitcast(E4M3X4),
                    lhsT_scale=row_scales[h][:, unit, :],
                    rhs=rhs,
                    rhs_scale=rhs_scale,
                    start=(k == 0),
                    stop=(k == PASSES - 1),
                )
            passes_done[key] = upto

        tau, work = {}, {}

        def pieces(key):
            step = N_TILE // 2 if key == TILES[-1] else N_TILE
            n0 = key[2] * N_TILE
            return [slice(c, c + step) for c in range(n0, n0 + N_TILE, step)]

        def store(rows, tiles, key):
            h, r, n = key
            if key in SINGLE_STORES:
                nc.sync.dma_start(out=rows[h][:, r, columns(n)], in_=tiles[h, r][:, columns(n)])
            elif n == N_TILES - 1:
                nc.sync.dma_start(out=rows[h][:, r, :], in_=tiles[h, r][:])

        def take_sum(key):
            h, r, n = key
            if (h, r) not in tau:
                tau_tile = stage.tile([P, N], F32, name="tau_tile")
                work_tile = stage.tile([P, N], F32, name="work_tile")
                tau[h, r] = tau_tile
                work[h, r] = work_tile
            bank = sums.pop(key)
            n0 = n * N_TILE
            for c in pieces(key):
                nc.scalar.copy(out=tau[h, r][:, c], in_=bank[:, c.start - n0 : c.stop - n0])
            store(tau_rows, tau, key)

        def subtract_u(key):
            h, r, n = key
            for c in pieces(key):
                nc.vector.tensor_tensor(out=work[h, r][:, c], in0=tau[h, r][:, c], in1=u_raw[h][:, r, c], op=SUB)

        def exponentiate(key):
            h, r, n = key
            for c in pieces(key):
                nc.scalar.activation(out=work[h, r][:, c], in_=work[h, r][:, c], func=EXP)

        def close(key):
            h, r, n = key
            for c in pieces(key):
                nc.vector.scalar_tensor_tensor(
                    out=work[h, r][:, c], in0=work[h, r][:, c], scalar=1.0, in1=tau[h, r][:, c], op0=SUB, op1=SUB
                )
            store(c_new_rows, work, key)

        vector_copy = nc.vector.tensor_copy
        scalar_copy = nc.scalar.copy
        half = N_TILE // 2

        for b in SU_BANKS:
            turn(0, b)
        for b in SU_BANKS:
            empty_turned(0, b, vector_copy)
        for b in SU_BANKS:
            quantize_rows(0, b)
        interleave(0, 1, vector_copy)
        turn(0, 2)
        turn(0, 3)
        interleave(0, 2, vector_copy, 0, half)
        empty_turned(0, 2, scalar_copy)
        empty_turned(0, 3, scalar_copy)
        interleave(0, 0, scalar_copy)
        quantize_sv(0, 1)
        quantize_rows(0, 2)
        quantize_rows(0, 3)
        interleave(0, 2, scalar_copy, half, N_TILE)
        turn(0, 4)
        for key in FIRST:
            multiply(key, SU_PASSES)
        empty_turned(0, 4, scalar_copy)
        quantize_sv(0, 0)
        interleave(1, 0, scalar_copy)
        for key in FIRST[:2]:
            multiply(key, SU_PASSES + 1)
        turn(1, 2)
        turn(1, 3)
        quantize_sv(0, 2)
        for key in FIRST[2:4]:
            multiply(key, SU_PASSES + 1)
        quantize_rows(0, 4)
        turn(1, 4)
        empty_turned(1, 2, scalar_copy)
        empty_turned(1, 3, scalar_copy)
        interleave(1, 1, vector_copy)
        empty_turned(1, 4, scalar_copy)
        interleave(1, 2, vector_copy)
        interleave(2, 1, scalar_copy)
        for n in range(N_TILES):
            quantize_sv(1, n)
        interleave(2, 0, vector_copy)
        quantize_sv(2, 0)
        for key in FIRST:
            multiply(key, PASSES - 1)
        interleave(2, 2, vector_copy)
        quantize_sv(2, 1)
        quantize_sv(2, 2)
        for b in (2, 3, 4):
            quantize_rows(1, b)

        exp_done, close_done = 0, 0
        for s in range(len(TILES) + LAST_LAG):
            later = LATER.get(s, [])
            for h, b in later:
                turn(h, b)
            if s < len(TILES):
                multiply(TILES[s], PASSES)
            for h, b in later:
                empty_turned(h, b, scalar_copy)
            lag = max(LAST_LAG, LAG - max(0, s - CATCH_UP))
            ready = max(0, min(len(TILES), s - lag + 1))
            for key in TILES[exp_done:ready]:
                exponentiate(key)
            exp_done = ready
            if 1 <= s <= len(TILES):
                subtract_u(TILES[s - 1])
            for h, b in later:
                quantize_rows(h, b)
            for key in TILES[close_done:ready]:
                close(key)
            close_done = ready
            if s < len(TILES):
                take_sum(TILES[s])
